import numpy as np
import ml_dtypes


def mxq(x, axis, fmt="e4m3"):
    dtype, down = {"e4m3": (ml_dtypes.float8_e4m3fn, 7), "e5m2": (ml_dtypes.float8_e5m2, 14)}[fmt]
    v = np.moveaxis(np.asarray(x, np.float32).astype(ml_dtypes.bfloat16).astype(np.float64), axis, -1)
    blocks = v.reshape(v.shape[:-1] + (-1, 32))
    amax = np.abs(blocks).max(-1, keepdims=True)
    byte = np.maximum(np.where(amax > 0, np.frexp(amax)[1] - 1 + 127, 0) - down, 1)
    scale = np.exp2(byte - 127.0)
    codes = (blocks / scale).astype(np.float32).astype(dtype).astype(np.float64)
    return np.moveaxis((codes * scale).reshape(v.shape), -1, axis)


WIDE = False


def mx_kscale(k):
    if not WIDE:
        return np.ones(k)
    levels = np.array([10, -10, 5, -5, 0])
    if k % 512:
        return np.exp2(np.random.permutation(np.resize(levels, k // 32))).repeat(32)
    a = np.empty((k // 512, 16))
    for p in range(k // 512):
        a[p, :8] = np.random.permutation(np.resize(levels, 8))
        for g in range(8):
            far = levels[np.abs(levels - a[p, g]) >= 10]
            a[p, g + 8] = far[np.random.randint(len(far))]
    return np.exp2(a.ravel()).repeat(32)


def f64(x):
    return np.asarray(x).astype(np.float64)


def striped(idx):
    return np.tile(idx.reshape(-1, 16).T, (8, 1)).astype(np.uint16)


def unstriped(offs):
    return offs[:16].T.reshape(-1).astype(np.int64)


E2M1 = np.array([0.0, 0.5, 1.0, 1.5, 2.0, 3.0, 4.0, 6.0, -0.0, -0.5, -1.0, -1.5, -2.0, -3.0, -4.0, -6.0])


def pack_weight(w, fmt):
    k, n = w.shape
    w = f64(np.asarray(w, np.float32).astype(ml_dtypes.bfloat16)).reshape(k // 32, 32, n)
    amax = np.abs(w).max(1)
    if fmt == "e4m3":
        byte = np.frexp(amax)[1] - 1 + 127 - 7
    else:
        mant, ex = np.frexp(amax / 6.0)
        byte = np.where(mant > 0.5, ex, ex - 1) + 127
    byte = np.clip(np.where(amax > 0, byte, 1), 1, 254)
    scaled = (w * np.exp2(127.0 - byte)[:, None, :]).reshape(k, n).astype(np.float32)
    by_word = np.ascontiguousarray(scaled.reshape(k // 512, 128, 4, n).transpose(0, 1, 3, 2))
    if fmt == "e4m3":
        words = by_word.astype(ml_dtypes.float8_e4m3fn).view(np.uint8)
    else:
        c = by_word.astype(ml_dtypes.float4_e2m1fn).view(np.uint8) & 0xF
        words = (c[..., 0::2] | (c[..., 1::2] << 4)).reshape(k // 512, 128, 2 * n)
    return np.ascontiguousarray(words), np.ascontiguousarray(byte.astype(np.uint8).reshape(k // 512, 16, n))


def unpack_weight(words, scales, fmt):
    g, _, n = scales.shape
    words = np.ascontiguousarray(words).reshape(g, 128, n, -1)
    if fmt == "e4m3":
        vals = words.view(ml_dtypes.float8_e4m3fn).astype(np.float64)
    else:
        nib = np.empty((g, 128, n, 4), np.uint8)
        nib[..., 0::2] = words & 0xF
        nib[..., 1::2] = words >> 4
        vals = E2M1[nib]
    vals = vals * np.repeat(np.exp2(scales.astype(np.float64) - 127.0), 8, axis=1)[..., None]
    return vals.transpose(0, 1, 3, 2).reshape(g * 512, n)


def gelu(v):
    return 0.5 * v * (1.0 + np.tanh(np.sqrt(2.0 / np.pi) * (v + 0.044715 * v**3)))


def striped8(idx):
    return np.concatenate([v.reshape(-1, 16).T for v in idx]).astype(np.uint16)


def unstriped8(offs):
    return np.stack([offs[16 * g:16 * g + 16].T.reshape(-1) for g in range(8)]).astype(np.int64)


def runs(v, idx8):
    k = np.arange(v.shape[0])
    return v[k[:, None], idx8[k % 512 // 64]]


T, S, T2, K, K2, H, N = 2048, 1024, 2048, 1024, 512, 1024, 512


def setup_inputs():
    n = np.random.standard_normal
    s = mx_kscale(K)[:, None]
    s2 = mx_kscale(K2)[:, None]
    u = mx_kscale(H)[:, None]
    tab_words, tab_scales = pack_weight(n((K, T)) * s, "e4m3")
    tab2_words, tab2_scales = pack_weight(n((K2, T)) * s2, "e4m3")
    w2_words, w2_scales = pack_weight(n((K2, H)) / np.sqrt(K2) / s2 * u.T, "e2m1")
    offs = striped8(np.stack([np.random.permutation(T)[:S] for _ in range(8)]))
    offs2 = striped(np.random.permutation(T)[:S])
    offs3 = striped(np.random.permutation(T2)[:S])
    return {
        "tab_words": tab_words, "tab_scales": tab_scales,
        "tab2_words": tab2_words, "tab2_scales": tab2_scales,
        "offs": offs, "offs2": offs2, "offs3": offs3,
        "w1": (n((K, H)) / np.sqrt(K) / s * u.T).astype(np.float32),
        "w2_words": w2_words, "w2_scales": w2_scales,
        "w3": (n((H, N)) / np.sqrt(H) / u).astype(np.float32),
        "rm": (0.8 * n((N, S))).astype(np.float32),
        "page1": n((N, T2)).astype(np.float32),
        "wgo": np.exp(0.3 * n((128, S))).astype(np.float32),
    }


def reference(tab_words, tab_scales, tab2_words, tab2_scales, offs, offs2, offs3,
              w1, w2_words, w2_scales, w3, rm, page1, wgo):
    v = runs(unpack_weight(tab_words, tab_scales, "e4m3"), unstriped8(offs))
    v2 = unpack_weight(tab2_words, tab2_scales, "e4m3")[:, unstriped(offs2)]
    w2 = unpack_weight(w2_words, w2_scales, "e2m1")
    a = mxq(f64(w1), 0, "e4m3").T @ v
    b = w2.T @ v2
    h = np.abs(np.maximum(a, b))
    e = mxq(f64(w3), 0, "e4m3").T @ mxq(h, 0, "e4m3")
    y = np.tanh(e + f64(rm))
    out = f64(page1).copy()
    out[:, unstriped(offs3)] = np.tile(f64(wgo), (N // 128, 1)) * y
    return out

@@ -1,0 +1,255 @@
+from contextlib import ExitStack
+
+import concourse.mybir as mybir
+
+T, S, T2, K, K2, H, N = 2048, 1024, 2048, 1024, 512, 1024, 512
+FLOPS = 2 * S * (K * H + K2 * H + H * N)
+
+F32 = mybir.dt.float32
+BF16 = mybir.dt.bfloat16
+I32 = mybir.dt.int32
+U32 = mybir.dt.uint32
+U16 = mybir.dt.uint16
+U8 = mybir.dt.uint8
+FP8X4 = mybir.dt.float8_e4m3fn_x4
+FP4X4 = mybir.dt.float4_e2m1fn_x4
+ALU = mybir.AluOpType
+ACT = mybir.ActivationFunctionType
+
+P = 128
+PACK = 4
+PASS = P * PACK
+SLICE = 256
+SLICES = S // SLICE
+GROUP = 16
+BANK = 512
+
+
+def tile_list_proof_impression_judge_kernel(
+    tc, tab_words, tab_scales, tab2_words, tab2_scales, offs, offs2, offs3,
+    w1, w2_words, w2_scales, w3, rm, page1, wgo, out,
+):
+    nc = tc.nc
+    with ExitStack() as ctx:
+        keep = ctx.enter_context(tc.tile_pool(name="keep", bufs=1))
+        ring = ctx.enter_context(tc.tile_pool(name="ring", bufs=2))
+        psum = ctx.enter_context(tc.psum_pool(name="psum", bufs=4))
+
+        def held(name, shape, dtype):
+            return keep.tile(shape, dtype, name=name, align_bytes=64)
+
+        def rows_tile(slot, name, shape, dtype=F32):
+            return keep.tile(shape, dtype, name=name, tag=f"rows_{slot}", align_bytes=64)
+
+        def load_words(slot, name, words):
+            window = rows_tile(slot, name, [P, T], U32)
+            nc.sync.dma_start(out=window[:].bitcast(I32), in_=words.rearrange("p t i -> p (t i)").bitcast(I32))
+            return window
+
+        def load_w1(slot, b, a, queue=nc.sync):
+            raw = rows_tile(slot, f"w1_raw_{b}{a}", [P, PACK, PASS])
+            rows = w1[a * PASS:(a + 1) * PASS, b * PASS:(b + 1) * PASS]
+            queue.dma_start(out=raw[:], in_=rows.rearrange("(p i) r -> p i r", i=PACK))
+            return raw
+
+        def load_w3(slot, b):
+            raw = rows_tile(slot, f"w3_raw_{b}", [P, PACK, N])
+            nc.sync.dma_start(out=raw[:], in_=w3[b * PASS:(b + 1) * PASS, :].rearrange("(p t) n -> p t n", t=PACK))
+            return raw
+
+        def load_plane(queue, tile_i32, scales):
+            for d in range(4):
+                queue.dma_start(out=tile_i32[32 * d:32 * d + 4, :], in_=scales[4 * d:4 * d + 4, :].bitcast(I32))
+
+        def gather(name, window, offsets, dtype, j0=0, j1=S):
+            picked = held(name, [P, j1 - j0], dtype)
+            nc.vector.tensor_copy(out=picked[:], in_=window[:].indirect(offsets[:, j0 // GROUP:j1 // GROUP]))
+            return picked
+
+        def quantise(name, values, width):
+            codes = held(f"{name}_codes", [P, width], U32)
+            scales = held(f"{name}_scales", [P, width], U8)
+            nc.vector.quantize_mx(out=codes[:].bitcast(FP8X4), scales=scales[:], in_=values[:])
+            return codes, scales
+
+        def after_paper(name, shape, s, b, pair):
+            return keep.tile(shape, F32, name=name, tag=f"paper_{s}{b}{pair}", align_bytes=64)
+
+        def load_f32(tile, rows):
+            nc.sync.dma_start(out=tile[:], in_=rows)
+            return tile
+
+        v_scale_window = held("v_scale_window", [P, T], U8)
+        nc.vector.memset(v_scale_window[:].bitcast(I32), 0)
+        v2_scale_window = held("v2_scale_window", [P, T], U8)
+        nc.vector.memset(v2_scale_window[:].bitcast(I32), 0)
+        w2_scale_raw = held("w2_scale_raw", [P, H // 4], I32)
+        nc.gpsimd.memset(w2_scale_raw[:], 0)
+
+        list1 = held("list1", [P, S // GROUP], U16)
+        nc.sync.dma_start(list1[:], offs)
+        list2 = held("list2", [P, S // GROUP], U16)
+        nc.sync.dma_start(list2[:], offs2)
+        for a in range(2):
+            nc.sync.dma_start(out=v_scale_window[:].bitcast(I32)[4 * a:P:8, :], in_=tab_scales[a].bitcast(I32))
+        w1_raw = {(0, 0): load_w1(1, 0, 0, nc.scalar)}
+        load_plane(nc.scalar, v2_scale_window[:].bitcast(I32), tab2_scales[0])
+        load_plane(nc.gpsimd, w2_scale_raw[:], w2_scales[0])
+        w1_raw[0, 1] = load_w1(2, 0, 1)
+        v2_window = load_words(0, "v2_window", tab2_words[0])
+        w1_raw[1, 0] = load_w1(5, 1, 0)
+        w2_raw = held("w2_raw", [P, H // 2], I32)
+        nc.sync.dma_start(out=w2_raw[:], in_=w2_words[0].bitcast(I32))
+        v_window = [load_words(3 + a, f"v_window_{a}", tab_words[a]) for a in range(2)]
+        w1_raw[1, 1] = load_w1(1, 1, 1)
+        w3_raw = [load_w3(2, 0), load_w3(0, 1)]
+        rm_rows = rm.rearrange("(c p) j -> p c j", p=P)
+        rm_first = load_f32(held("rm_first", [P, N // P, SLICE], F32), rm_rows[:, :, 0:SLICE])
+        gain = load_f32(held("gain", [P, S], F32), wgo)
+        list3 = held("list3", [P, S // GROUP], U16)
+        nc.sync.dma_start(list3[:], offs3)
+        page = [load_f32(rows_tile((5, 3, 4, 1)[c], f"page_{c}", [P, T2]), page1[c * P:(c + 1) * P, :]) for c in range(N // P)]
+        rm_rest = [load_f32(held(f"rm_rest_{c}", [P, S - SLICE], F32), rm_rows[:, c, SLICE:S]) for c in range(N // P)]
+
+        HALF = S // 2
+        v_scales_picked = gather("v_scales_picked", v_scale_window, list1, U8)
+        v_scales = held("v_scales", [P, S], U8)
+        nc.vector.tensor_copy(out=v_scales[:].bitcast(I32), in_=v_scales_picked[:].bitcast(I32))
+        for a in range(2):
+            for row in range(1, 4):
+                nc.scalar.dma_start(
+                    out=v_scales[:].bitcast(I32)[4 * a + row:P:32, :],
+                    in_=v_scales_picked[:].bitcast(I32)[4 * a + 8 * row:P:32, :],
+                )
+        v2_scales = [gather("v2_scales_0", v2_scale_window, list2, U8, 0, HALF)]
+        v2_codes = [gather("v2_codes_0", v2_window, list2, U32, 0, HALF)]
+        w2_codes = held("w2_codes", [P, 2 * H], U8)
+        nc.vector.tensor_copy(
+            out=w2_codes[:].bitcast(U16).rearrange("p (b t m) -> p b m t", b=2, t=PACK),
+            in_=w2_raw[:].bitcast(U16).rearrange("p (b m t) -> p b m t", b=2, t=PACK),
+        )
+        w2_plane = held("w2_plane", [P, H], U8)
+        nc.vector.tensor_copy(
+            out=w2_plane[:].rearrange("p (b t m) -> p b m t", b=2, t=PACK),
+            in_=w2_scale_raw[:].bitcast(U8).rearrange("p (b m t) -> p b m t", b=2, t=PACK),
+        )
+        v2_scales.append(gather("v2_scales_1", v2_scale_window, list2, U8, HALF, S))
+        v2_codes.append(gather("v2_codes_1", v2_window, list2, U32, HALF, S))
+
+        w1_q, paper, h_q = {}, {}, {}
+
+        def quantise_w1(b, a):
+            for pair in range(2):
+                rounded = ring.tile([P, 2 * PASS], BF16, name="w1_rounded", bufs=8, align_bytes=64)
+                nc.scalar.copy(
+                    out=rounded[:].rearrange("p (t m i) -> p m i t", t=2, i=PACK),
+                    in_=w1_raw[b, a][:].rearrange("p i (m t) -> p m i t", t=PACK)[:, :, :, 2 * pair:2 * pair + 2],
+                )
+                w1_q[b, a, pair] = quantise(f"w1_{b}{a}{pair}", rounded, 2 * P)
+
+        def quantise_w3(b):
+            rounded = ring.tile([P, PACK * N], BF16, name="w3_rounded", bufs=2, align_bytes=64)
+            nc.vector.tensor_copy(
+                out=rounded[:].rearrange("p (c i t) -> p c t i", i=4, t=PACK),
+                in_=w3_raw[b][:].rearrange("p t (c i) -> p c t i", i=4),
+            )
+            return quantise(f"w3_{b}", rounded, N)
+
+        def paper_readings(s, b):
+            cols = slice(s % 2 * SLICE, (s % 2 + 1) * SLICE)
+            for pair in range(2):
+                bank = psum.tile([P, 2, SLICE], F32, name="lone_bank")
+                for t in range(2):
+                    r0 = b * PASS + (2 * pair + t) * P
+                    nc.tensor.matmul_mx(
+                        out=bank[:, t, :],
+                        lhsT=w2_codes[:, 2 * r0:2 * (r0 + P)].bitcast(FP4X4), lhsT_scale=w2_plane[:, r0:r0 + P],
+                        rhs=v2_codes[s // 2][:, cols].bitcast(FP8X4), rhs_scale=v2_scales[s // 2][:, cols],
+                        start=True, stop=True,
+                    )
+                paper[s, b, pair] = after_paper(f"paper_{s}{b}{pair}", [P, SLICE, 2], s, b, pair)
+                nc.scalar.copy(out=paper[s, b, pair][:], in_=bank[:].rearrange("p t j -> p j t"))
+
+        def larger_reading(s, b):
+            cols = slice(s * SLICE, (s + 1) * SLICE)
+            larger = ring.tile([P, 2, SLICE, 2], F32, name="larger", bufs=4)
+            for pair in range(2):
+                bank = psum.tile([P, 2, SLICE], F32, name="sort_bank")
+                for t in range(2):
+                    for a in range(2):
+                        codes, scales = w1_q[b, a, pair]
+                        nc.tensor.matmul_mx(
+                            out=bank[:, t, :],
+                            lhsT=codes[:, t * P:(t + 1) * P].bitcast(FP8X4), lhsT_scale=scales[:, t * P:(t + 1) * P],
+                            rhs=v_codes[a, s // 2][:, s % 2 * SLICE:(s % 2 + 1) * SLICE].bitcast(FP8X4), rhs_scale=v_scales[4 * a:P, cols],
+                            start=(a == 0), stop=(a == 1),
+                        )
+                nc.vector.tensor_tensor(
+                    out=larger[:, pair, :, :], in0=bank[:].rearrange("p t j -> p j t"), in1=paper[s, b, pair][:], op=ALU.max,
+                )
+            return larger
+
+        def quantise_h(s, b, larger):
+            h = ring.tile([P, PACK * SLICE], BF16, name="h", bufs=4, align_bytes=64)
+            nc.scalar.activation(
+                out=h[:].rearrange("p (j pair t) -> p j pair t", pair=2, t=2),
+                in_=larger[:].rearrange("p pair j t -> p j pair t"), func=ACT.Abs,
+            )
+            h_q[s, b] = quantise(f"h_{s}{b}", h, SLICE)
+
+        def features(parts, residual):
+            width = len(parts) * SLICE
+            summed = ring.tile([P, width], F32, name="summed")
+            for first in range(0, len(parts), 2):
+                here = parts[first:first + 2]
+                bank = psum.tile([P, BANK], F32, name="lone_bank")
+                for i, (c, s) in enumerate(here):
+                    for b in range(2):
+                        nc.tensor.matmul_mx(
+                            out=bank[:, i * SLICE:(i + 1) * SLICE],
+                            lhsT=w3_q[b][0][:, c * P:(c + 1) * P].bitcast(FP8X4), lhsT_scale=w3_q[b][1][:, c * P:(c + 1) * P],
+                            rhs=h_q[s, b][0][:].bitcast(FP8X4), rhs_scale=h_q[s, b][1][:],
+                            start=(b == 0), stop=(b == 1),
+                        )
+                cols = slice(first * SLICE, (first + len(here)) * SLICE)
+                nc.vector.tensor_tensor(out=summed[:, cols], in0=bank[:, 0:len(here) * SLICE], in1=residual[:, cols], op=ALU.add)
+            y = ring.tile([P, width], F32, name="y", bufs=3)
+            nc.scalar.activation(out=y[:], in_=summed[:], func=ACT.Tanh)
+            return y
+
+        def place(c, values, gain, j0, j1):
+            nc.vector.tensor_tensor(
+                out=page[c][:].indirect(list3[:, j0 // GROUP:j1 // GROUP]), in0=values, in1=gain, op=ALU.mult,
+            )
+
+        quantise_w1(0, 0)
+        quantise_w1(0, 1)
+        quantise_w1(1, 0)
+        v_codes = {(a, h): gather(f"v_codes_{a}{h}", v_window[a], list1, U32, h * HALF, (h + 1) * HALF) for a in range(2) for h in range(2)}
+        paper_readings(0, 0)
+        paper_readings(0, 1)
+        quantise_w1(1, 1)
+        paper_readings(1, 0)
+        paper_readings(1, 1)
+        quantise_h(0, 0, larger_reading(0, 0))
+        quantise_h(0, 1, larger_reading(0, 1))
+        w3_q = [quantise_w3(b) for b in range(2)]
+        rm_first_flat = rm_first[:].rearrange("p c j -> p (c j)")
+        y_first = [features([(c, 0), (c + 1, 0)], rm_first_flat[:, c * SLICE:(c + 2) * SLICE]) for c in (0, 2)]
+        for s in range(1, SLICES):
+            if s + 1 < SLICES:
+                paper_readings(s + 1, 0)
+                paper_readings(s + 1, 1)
+            quantise_h(s, 0, larger_reading(s, 0))
+            quantise_h(s, 1, larger_reading(s, 1))
+            c = s - 1
+            place(c, y_first[c // 2][:, c % 2 * SLICE:(c % 2 + 1) * SLICE], gain[:, 0:SLICE], 0, SLICE)
+        rest = range(1, SLICES)
+        y_rest = features([(0, s) for s in rest], rm_rest[0][:])
+        place(3, y_first[1][:, SLICE:2 * SLICE], gain[:, 0:SLICE], 0, SLICE)
+        for c in range(N // P):
+            y_here = y_rest
+            if c + 1 < N // P:
+                y_rest = features([(c + 1, s) for s in rest], rm_rest[c + 1][:])
+            place(c, y_here[:], gain[:, SLICE:S], SLICE, S)
+            nc.sync.dma_start(out=out[c * P:(c + 1) * P, :], in_=page[c][:])

@@ -1,6 +1,7 @@
 from contextlib import ExitStack
 
 import concourse.mybir as mybir
+from concourse.masks import make_identity
 
 T, S, T2, K, K2, H, N = 2048, 1024, 2048, 1024, 512, 1024, 512
 FLOPS = 2 * S * (K * H + K2 * H + H * N)
@@ -91,11 +92,11 @@ def tile_list_proof_impression_judge_kernel(
         list2 = held("list2", [P, S // GROUP], U16)
         nc.sync.dma_start(list2[:], offs2)
         for a in range(2):
-            nc.sync.dma_start(out=v_scale_window[:].bitcast(I32)[4 * a:P:8, :], in_=tab_scales[a].bitcast(I32))
-        w1_raw = {(0, 0): load_w1(1, 0, 0, nc.scalar)}
+            for r in range(2):
+                nc.scalar.dma_start(out=v_scale_window[:].bitcast(I32)[4 * a + r:P:GROUP, :], in_=tab_scales[a, r:16:2, :].bitcast(I32))
         load_plane(nc.scalar, v2_scale_window[:].bitcast(I32), tab2_scales[0])
         load_plane(nc.gpsimd, w2_scale_raw[:], w2_scales[0])
-        w1_raw[0, 1] = load_w1(2, 0, 1)
+        w1_raw = {(0, 0): load_w1(1, 0, 0), (0, 1): load_w1(2, 0, 1)}
         v2_window = load_words(0, "v2_window", tab2_words[0])
         w1_raw[1, 0] = load_w1(5, 1, 0)
         w2_raw = held("w2_raw", [P, H // 2], I32)
@@ -104,22 +105,26 @@ def tile_list_proof_impression_judge_kernel(
         w1_raw[1, 1] = load_w1(1, 1, 1)
         w3_raw = [load_w3(2, 0), load_w3(0, 1)]
         rm_rows = rm.rearrange("(c p) j -> p c j", p=P)
-        rm_first = load_f32(held("rm_first", [P, N // P, SLICE], F32), rm_rows[:, :, 0:SLICE])
+        rm_slice = [load_f32(held("rm_slice_0", [P, N // P, SLICE], F32), rm_rows[:, :, 0:SLICE])]
         gain = load_f32(held("gain", [P, S], F32), wgo)
         list3 = held("list3", [P, S // GROUP], U16)
         nc.sync.dma_start(list3[:], offs3)
-        page = [load_f32(rows_tile((5, 3, 4, 1)[c], f"page_{c}", [P, T2]), page1[c * P:(c + 1) * P, :]) for c in range(N // P)]
-        rm_rest = [load_f32(held(f"rm_rest_{c}", [P, S - SLICE], F32), rm_rows[:, c, SLICE:S]) for c in range(N // P)]
+        page = [load_f32(rows_tile(5, "page_0", [P, T2]), page1[0:P, :])]
+        rm_slice.append(load_f32(held("rm_slice_1", [P, N // P, SLICE], F32), rm_rows[:, :, SLICE:2 * SLICE]))
+        page += [load_f32(rows_tile((5, 3, 4, 1)[c], f"page_{c}", [P, T2]), page1[c * P:(c + 1) * P, :]) for c in range(1, N // P)]
+        rm_rest = load_f32(held("rm_rest", [P, N // P, S // 2], F32), rm_rows[:, :, S // 2:S])
+        identity = held("identity", [P, P], F32)
+        make_identity(nc, identity[:])
 
         HALF = S // 2
         v_scales_picked = gather("v_scales_picked", v_scale_window, list1, U8)
         v_scales = held("v_scales", [P, S], U8)
         nc.vector.tensor_copy(out=v_scales[:].bitcast(I32), in_=v_scales_picked[:].bitcast(I32))
         for a in range(2):
-            for row in range(1, 4):
+            for r in range(2):
                 nc.scalar.dma_start(
-                    out=v_scales[:].bitcast(I32)[4 * a + row:P:32, :],
-                    in_=v_scales_picked[:].bitcast(I32)[4 * a + 8 * row:P:32, :],
+                    out=v_scales[:].bitcast(I32)[4 * a + 2 + r:P:32, :],
+                    in_=v_scales_picked[:].bitcast(I32)[4 * a + GROUP + r:P:32, :],
                 )
         v2_scales = [gather("v2_scales_0", v2_scale_window, list2, U8, 0, HALF)]
         v2_codes = [gather("v2_codes_0", v2_window, list2, U32, 0, HALF)]
@@ -128,19 +133,19 @@ def tile_list_proof_impression_judge_kernel(
             out=w2_codes[:].bitcast(U16).rearrange("p (b t m) -> p b m t", b=2, t=PACK),
             in_=w2_raw[:].bitcast(U16).rearrange("p (b m t) -> p b m t", b=2, t=PACK),
         )
-        w2_plane = held("w2_plane", [P, H], U8)
+        v2_scales.append(gather("v2_scales_1", v2_scale_window, list2, U8, HALF, S))
+        v2_codes.append(gather("v2_codes_1", v2_window, list2, U32, HALF, S))
+        w2_plane = keep.tile([P, H], U8, name="w2_plane", tag="v2_scale_window", align_bytes=64)
         nc.vector.tensor_copy(
             out=w2_plane[:].rearrange("p (b t m) -> p b m t", b=2, t=PACK),
             in_=w2_scale_raw[:].bitcast(U8).rearrange("p (b m t) -> p b m t", b=2, t=PACK),
         )
-        v2_scales.append(gather("v2_scales_1", v2_scale_window, list2, U8, HALF, S))
-        v2_codes.append(gather("v2_codes_1", v2_window, list2, U32, HALF, S))
 
-        w1_q, paper, h_q = {}, {}, {}
+        w1_q, paper, h_q, product_t = {}, {}, {}, {}
 
         def quantise_w1(b, a):
             for pair in range(2):
-                rounded = ring.tile([P, 2 * PASS], BF16, name="w1_rounded", bufs=8, align_bytes=64)
+                rounded = ring.tile([P, 2 * PASS], BF16, name="w1_rounded", bufs=6, align_bytes=64)
                 nc.scalar.copy(
                     out=rounded[:].rearrange("p (t m i) -> p m i t", t=2, i=PACK),
                     in_=w1_raw[b, a][:].rearrange("p i (m t) -> p m i t", t=PACK)[:, :, :, 2 * pair:2 * pair + 2],
@@ -158,7 +163,7 @@ def tile_list_proof_impression_judge_kernel(
         def paper_readings(s, b):
             cols = slice(s % 2 * SLICE, (s % 2 + 1) * SLICE)
             for pair in range(2):
-                bank = psum.tile([P, 2, SLICE], F32, name="lone_bank")
+                bank = psum.tile([P, 2, SLICE], F32, name="paper_bank", bufs=2)
                 for t in range(2):
                     r0 = b * PASS + (2 * pair + t) * P
                     nc.tensor.matmul_mx(
@@ -167,14 +172,14 @@ def tile_list_proof_impression_judge_kernel(
                         rhs=v2_codes[s // 2][:, cols].bitcast(FP8X4), rhs_scale=v2_scales[s // 2][:, cols],
                         start=True, stop=True,
                     )
-                paper[s, b, pair] = after_paper(f"paper_{s}{b}{pair}", [P, SLICE, 2], s, b, pair)
-                nc.scalar.copy(out=paper[s, b, pair][:], in_=bank[:].rearrange("p t j -> p j t"))
+                paper[s, b, pair] = after_paper(f"paper_{s}{b}{pair}", [P, 2, SLICE], s, b, pair)
+                nc.scalar.copy(out=paper[s, b, pair][:], in_=bank[:])
 
         def larger_reading(s, b):
             cols = slice(s * SLICE, (s + 1) * SLICE)
-            larger = ring.tile([P, 2, SLICE, 2], F32, name="larger", bufs=4)
+            larger = ring.tile([P, PACK, SLICE], F32, name="larger", bufs=4)
             for pair in range(2):
-                bank = psum.tile([P, 2, SLICE], F32, name="sort_bank")
+                bank = psum.tile([P, 2, SLICE], F32, name="sort_bank", bufs=3)
                 for t in range(2):
                     for a in range(2):
                         codes, scales = w1_q[b, a, pair]
@@ -185,42 +190,63 @@ def tile_list_proof_impression_judge_kernel(
                             start=(a == 0), stop=(a == 1),
                         )
                 nc.vector.tensor_tensor(
-                    out=larger[:, pair, :, :], in0=bank[:].rearrange("p t j -> p j t"), in1=paper[s, b, pair][:], op=ALU.max,
+                    out=larger[:, 2 * pair:2 * pair + 2, :], in0=bank[:], in1=paper[s, b, pair][:], op=ALU.max,
                 )
             return larger
 
         def quantise_h(s, b, larger):
             h = ring.tile([P, PACK * SLICE], BF16, name="h", bufs=4, align_bytes=64)
             nc.scalar.activation(
-                out=h[:].rearrange("p (j pair t) -> p j pair t", pair=2, t=2),
-                in_=larger[:].rearrange("p pair j t -> p j pair t"), func=ACT.Abs,
+                out=h[:].rearrange("p (c i t) -> p c t i", i=2, t=PACK),
+                in_=larger[:].rearrange("p t (c i) -> p c t i", i=2), func=ACT.Abs,
             )
             h_q[s, b] = quantise(f"h_{s}{b}", h, SLICE)
 
-        def features(parts, residual):
-            width = len(parts) * SLICE
-            summed = ring.tile([P, width], F32, name="summed")
-            for first in range(0, len(parts), 2):
-                here = parts[first:first + 2]
-                bank = psum.tile([P, BANK], F32, name="lone_bank")
-                for i, (c, s) in enumerate(here):
-                    for b in range(2):
-                        nc.tensor.matmul_mx(
-                            out=bank[:, i * SLICE:(i + 1) * SLICE],
-                            lhsT=w3_q[b][0][:, c * P:(c + 1) * P].bitcast(FP8X4), lhsT_scale=w3_q[b][1][:, c * P:(c + 1) * P],
-                            rhs=h_q[s, b][0][:].bitcast(FP8X4), rhs_scale=h_q[s, b][1][:],
-                            start=(b == 0), stop=(b == 1),
-                        )
-                cols = slice(first * SLICE, (first + len(here)) * SLICE)
-                nc.vector.tensor_tensor(out=summed[:, cols], in0=bank[:, 0:len(here) * SLICE], in1=residual[:, cols], op=ALU.add)
-            y = ring.tile([P, width], F32, name="y", bufs=3)
-            nc.scalar.activation(out=y[:], in_=summed[:], func=ACT.Tanh)
+        def second_product(s):
+            for half in range(2):
+                cols = slice(half * P, (half + 1) * P)
+                bank = psum.tile([P, N], F32, name="late_bank", bufs=3)
+                for b in range(2):
+                    nc.tensor.matmul_mx(
+                        out=bank[:],
+                        lhsT=h_q[s, b][0][:, cols].bitcast(FP8X4), lhsT_scale=h_q[s, b][1][:, cols],
+                        rhs=w3_q[b][0][:].bitcast(FP8X4), rhs_scale=w3_q[b][1][:],
+                        start=(b == 0), stop=(b == 1),
+                    )
+                product_t[2 * s + half] = held(f"product_t_{s}{half}", [P, N], F32)
+                nc.scalar.copy(out=product_t[2 * s + half][:], in_=bank[:])
+
+        def turn_residual(residual):
+            bank = psum.tile([P, BANK], F32, name="late_bank", bufs=3)
+            for i in range(BANK // P):
+                nc.tensor.transpose(bank[:, i * P:(i + 1) * P], residual[:, i * P:(i + 1) * P], identity[:])
+            residual_t = ring.tile([P, BANK], F32, name="residual_t", bufs=4)
+            nc.scalar.copy(out=residual_t[:], in_=bank[:])
+            return residual_t
+
+        def features(blocks, residual_t, y):
+            bank = psum.tile([P, BANK], F32, name="late_bank", bufs=3)
+            for i, (c, jt) in enumerate(blocks):
+                cols = slice(i * P, (i + 1) * P)
+                nc.tensor.matmul(bank[:, cols], residual_t[:, cols], identity[:], start=True, stop=False, is_transpose=True)
+                nc.tensor.matmul(bank[:, cols], product_t[jt][:, c * P:(c + 1) * P], identity[:], start=False, stop=True, is_transpose=True)
+            nc.scalar.activation(out=y[:], in_=bank[:], func=ACT.Tanh)
             return y
 
         def place(c, values, gain, j0, j1):
             nc.vector.tensor_tensor(
                 out=page[c][:].indirect(list3[:, j0 // GROUP:j1 // GROUP]), in0=values, in1=gain, op=ALU.mult,
             )
+
+        def slice_residual(s):
+            flat = rm_slice[s][:].rearrange("p c j -> p (c j)")
+            return [turn_residual(flat[:, i * BANK:(i + 1) * BANK]) for i in range(2)]
+
+        def slice_features(s, residual_t, y):
+            return [features([(c, 2 * s + half) for c in (2 * i, 2 * i + 1) for half in range(2)], residual_t[i], y[i]) for i in range(2)]
+
+        def place_slice(s, c, y):
+            place(c, y[c // 2][:, c % 2 * SLICE:(c % 2 + 1) * SLICE], gain[:, s * SLICE:(s + 1) * SLICE], s * SLICE, (s + 1) * SLICE)
 
         quantise_w1(0, 0)
         quantise_w1(0, 1)
@@ -234,22 +260,22 @@ def tile_list_proof_impression_judge_kernel(
         quantise_h(0, 0, larger_reading(0, 0))
         quantise_h(0, 1, larger_reading(0, 1))
         w3_q = [quantise_w3(b) for b in range(2)]
-        rm_first_flat = rm_first[:].rearrange("p c j -> p (c j)")
-        y_first = [features([(c, 0), (c + 1, 0)], rm_first_flat[:, c * SLICE:(c + 2) * SLICE]) for c in (0, 2)]
-        for s in range(1, SLICES):
-            if s + 1 < SLICES:
-                paper_readings(s + 1, 0)
-                paper_readings(s + 1, 1)
-            quantise_h(s, 0, larger_reading(s, 0))
-            quantise_h(s, 1, larger_reading(s, 1))
-            c = s - 1
-            place(c, y_first[c // 2][:, c % 2 * SLICE:(c % 2 + 1) * SLICE], gain[:, 0:SLICE], 0, SLICE)
-        rest = range(1, SLICES)
-        y_rest = features([(0, s) for s in rest], rm_rest[0][:])
-        place(3, y_first[1][:, SLICE:2 * SLICE], gain[:, 0:SLICE], 0, SLICE)
+        second_product(0)
+        y_slice = [slice_features(0, slice_residual(0), [ring.tile([P, BANK], F32, name="y", bufs=3) for i in range(2)])]
+        quantise_h(1, 0, larger_reading(1, 0))
+        quantise_h(1, 1, larger_reading(1, 1))
+        second_product(1)
+        for s in range(2):
+            for b in range(2):
+                paper_readings(s + 2, b)
+                quantise_h(s + 2, b, larger_reading(s + 2, b))
+        y_slice.append(slice_features(1, slice_residual(1), [after_paper(f"y_1{b}", [P, BANK], 3, b, 1) for b in range(2)]))
+        second_product(2)
+        second_product(3)
+        for s in range(2):
+            for c in range(N // P):
+                place_slice(s, c, y_slice[s])
         for c in range(N // P):
-            y_here = y_rest
-            if c + 1 < N // P:
-                y_rest = features([(c + 1, s) for s in rest], rm_rest[c + 1][:])
-            place(c, y_here[:], gain[:, SLICE:S], SLICE, S)
+            y = features([(c, jt) for jt in range(4, 8)], turn_residual(rm_rest[:, c, :]), ring.tile([P, BANK], F32, name="y", bufs=3))
+            place(c, y[:], gain[:, HALF:S], HALF, S)
             nc.sync.dma_start(out=out[c * P:(c + 1) * P, :], in_=page[c][:])

@@ -55,7 +55,9 @@ def tile_list_proof_impression_judge_kernel(
 
         def load_w3(slot, b):
             raw = rows_tile(slot, f"w3_raw_{b}", [P, PACK, N])
-            nc.sync.dma_start(out=raw[:], in_=w3[b * PASS:(b + 1) * PASS, :].rearrange("(p t) n -> p t n", t=PACK))
+            rows = w3[b * PASS:(b + 1) * PASS, :].rearrange("(u t e) n -> e u t n", t=PACK, e=2)
+            for e in range(2):
+                nc.sync.dma_start(out=raw[e:P:2, :, :], in_=rows[e])
             return raw
 
         def load_plane(queue, tile_i32, scales):
@@ -80,24 +82,25 @@ def tile_list_proof_impression_judge_kernel(
             nc.sync.dma_start(out=tile[:], in_=rows)
             return tile
 
-        v_scale_window = held("v_scale_window", [P, T], U8)
-        nc.vector.memset(v_scale_window[:].bitcast(I32), 0)
         v2_scale_window = held("v2_scale_window", [P, T], U8)
         nc.vector.memset(v2_scale_window[:].bitcast(I32), 0)
+        v_scale_window = held("v_scale_window", [P, T], U8)
+        nc.vector.memset(v_scale_window[:].bitcast(I32), 0)
         w2_scale_raw = held("w2_scale_raw", [P, H // 4], I32)
         nc.gpsimd.memset(w2_scale_raw[:], 0)
 
-        list1 = held("list1", [P, S // GROUP], U16)
-        nc.sync.dma_start(list1[:], offs)
         list2 = held("list2", [P, S // GROUP], U16)
         nc.sync.dma_start(list2[:], offs2)
+        v2_window = load_words(0, "v2_window", tab2_words[0])
+        w1_raw = {(0, 0): load_w1(1, 0, 0)}
+        list1 = held("list1", [P, S // GROUP], U16)
+        nc.sync.dma_start(list1[:], offs)
+        load_plane(nc.scalar, v2_scale_window[:].bitcast(I32), tab2_scales[0])
         for a in range(2):
             for r in range(2):
                 nc.scalar.dma_start(out=v_scale_window[:].bitcast(I32)[4 * a + r:P:GROUP, :], in_=tab_scales[a, r:16:2, :].bitcast(I32))
-        load_plane(nc.scalar, v2_scale_window[:].bitcast(I32), tab2_scales[0])
         load_plane(nc.gpsimd, w2_scale_raw[:], w2_scales[0])
-        w1_raw = {(0, 0): load_w1(1, 0, 0), (0, 1): load_w1(2, 0, 1)}
-        v2_window = load_words(0, "v2_window", tab2_words[0])
+        w1_raw[0, 1] = load_w1(2, 0, 1)
         w1_raw[1, 0] = load_w1(5, 1, 0)
         w2_raw = held("w2_raw", [P, H // 2], I32)
         nc.sync.dma_start(out=w2_raw[:], in_=w2_words[0].bitcast(I32))
@@ -117,28 +120,20 @@ def tile_list_proof_impression_judge_kernel(
         make_identity(nc, identity[:])
 
         HALF = S // 2
+        v2_codes = [gather(f"v2_codes_{h}", v2_window, list2, U32, h * HALF, (h + 1) * HALF) for h in range(2)]
+        v2_scales = [gather(f"v2_scales_{h}", v2_scale_window, list2, U8, h * HALF, (h + 1) * HALF) for h in range(2)]
         v_scales_picked = gather("v_scales_picked", v_scale_window, list1, U8)
         v_scales = held("v_scales", [P, S], U8)
         nc.vector.tensor_copy(out=v_scales[:].bitcast(I32), in_=v_scales_picked[:].bitcast(I32))
-        for a in range(2):
-            for r in range(2):
-                nc.scalar.dma_start(
-                    out=v_scales[:].bitcast(I32)[4 * a + 2 + r:P:32, :],
-                    in_=v_scales_picked[:].bitcast(I32)[4 * a + GROUP + r:P:32, :],
-                )
-        v2_scales = [gather("v2_scales_0", v2_scale_window, list2, U8, 0, HALF)]
-        v2_codes = [gather("v2_codes_0", v2_window, list2, U32, 0, HALF)]
         w2_codes = held("w2_codes", [P, 2 * H], U8)
         nc.vector.tensor_copy(
-            out=w2_codes[:].bitcast(U16).rearrange("p (b t m) -> p b m t", b=2, t=PACK),
-            in_=w2_raw[:].bitcast(U16).rearrange("p (b m t) -> p b m t", b=2, t=PACK),
+            out=w2_codes[:].bitcast(I32).rearrange("p (b t u) -> p b t u", b=2, t=PACK),
+            in_=w2_raw[:].rearrange("p (b u t) -> p b t u", b=2, t=PACK),
         )
-        v2_scales.append(gather("v2_scales_1", v2_scale_window, list2, U8, HALF, S))
-        v2_codes.append(gather("v2_codes_1", v2_window, list2, U32, HALF, S))
-        w2_plane = keep.tile([P, H], U8, name="w2_plane", tag="v2_scale_window", align_bytes=64)
+        w2_plane = keep.tile([P, H], U8, name="w2_plane", tag="v_scale_window", align_bytes=64)
         nc.vector.tensor_copy(
-            out=w2_plane[:].rearrange("p (b t m) -> p b m t", b=2, t=PACK),
-            in_=w2_scale_raw[:].bitcast(U8).rearrange("p (b m t) -> p b m t", b=2, t=PACK),
+            out=w2_plane[:].bitcast(U16).rearrange("p (b t u) -> p b t u", b=2, t=PACK),
+            in_=w2_scale_raw[:].bitcast(U16).rearrange("p (b u t) -> p b t u", b=2, t=PACK),
         )
 
         w1_q, paper, h_q, product_t = {}, {}, {}, {}
@@ -147,8 +142,8 @@ def tile_list_proof_impression_judge_kernel(
             for pair in range(2):
                 rounded = ring.tile([P, 2 * PASS], BF16, name="w1_rounded", bufs=6, align_bytes=64)
                 nc.scalar.copy(
-                    out=rounded[:].rearrange("p (t m i) -> p m i t", t=2, i=PACK),
-                    in_=w1_raw[b, a][:].rearrange("p i (m t) -> p m i t", t=PACK)[:, :, :, 2 * pair:2 * pair + 2],
+                    out=rounded[:].rearrange("p (t u e i) -> p t u i e", t=2, e=2, i=PACK),
+                    in_=w1_raw[b, a][:].rearrange("p i (u t e) -> p t u i e", t=PACK, e=2)[:, 2 * pair:2 * pair + 2, :, :, :],
                 )
                 w1_q[b, a, pair] = quantise(f"w1_{b}{a}{pair}", rounded, 2 * P)
 
@@ -163,7 +158,7 @@ def tile_list_proof_impression_judge_kernel(
         def paper_readings(s, b):
             cols = slice(s % 2 * SLICE, (s % 2 + 1) * SLICE)
             for pair in range(2):
-                bank = psum.tile([P, 2, SLICE], F32, name="paper_bank", bufs=2)
+                bank = psum.tile([P, 2, SLICE], F32, name="paper_bank", bufs=3)
                 for t in range(2):
                     r0 = b * PASS + (2 * pair + t) * P
                     nc.tensor.matmul_mx(
@@ -205,7 +200,7 @@ def tile_list_proof_impression_judge_kernel(
         def second_product(s):
             for half in range(2):
                 cols = slice(half * P, (half + 1) * P)
-                bank = psum.tile([P, N], F32, name="late_bank", bufs=3)
+                bank = psum.tile([P, N], F32, name="late_bank", bufs=2)
                 for b in range(2):
                     nc.tensor.matmul_mx(
                         out=bank[:],
@@ -217,7 +212,7 @@ def tile_list_proof_impression_judge_kernel(
                 nc.scalar.copy(out=product_t[2 * s + half][:], in_=bank[:])
 
         def turn_residual(residual):
-            bank = psum.tile([P, BANK], F32, name="late_bank", bufs=3)
+            bank = psum.tile([P, BANK], F32, name="late_bank", bufs=2)
             for i in range(BANK // P):
                 nc.tensor.transpose(bank[:, i * P:(i + 1) * P], residual[:, i * P:(i + 1) * P], identity[:])
             residual_t = ring.tile([P, BANK], F32, name="residual_t", bufs=4)
@@ -225,7 +220,7 @@ def tile_list_proof_impression_judge_kernel(
             return residual_t
 
         def features(blocks, residual_t, y):
-            bank = psum.tile([P, BANK], F32, name="late_bank", bufs=3)
+            bank = psum.tile([P, BANK], F32, name="late_bank", bufs=2)
             for i, (c, jt) in enumerate(blocks):
                 cols = slice(i * P, (i + 1) * P)
                 nc.tensor.matmul(bank[:, cols], residual_t[:, cols], identity[:], start=True, stop=False, is_transpose=True)
@@ -233,17 +228,27 @@ def tile_list_proof_impression_judge_kernel(
             nc.scalar.activation(out=y[:], in_=bank[:], func=ACT.Tanh)
             return y
 
+        def slice_features(s, y):
+            for i in range(2):
+                bank = psum.tile([P, 2, SLICE], F32, name="late_bank", bufs=2)
+                for k in range(2):
+                    cols = slice((2 * i + k) * P, (2 * i + k + 1) * P)
+                    for b in range(2):
+                        nc.tensor.matmul_mx(
+                            out=bank[:, k, :],
+                            lhsT=w3_q[b][0][:, cols].bitcast(FP8X4), lhsT_scale=w3_q[b][1][:, cols],
+                            rhs=h_q[s, b][0][:].bitcast(FP8X4), rhs_scale=h_q[s, b][1][:],
+                            start=(b == 0), stop=(b == 1),
+                        )
+                summed = ring.tile([P, 2, SLICE], F32, name="summed")
+                nc.vector.tensor_tensor(out=summed[:], in0=bank[:], in1=rm_slice[s][:, 2 * i:2 * i + 2, :], op=ALU.add)
+                nc.scalar.activation(out=y[i][:], in_=summed[:].rearrange("p k j -> p (k j)"), func=ACT.Tanh)
+            return y
+
         def place(c, values, gain, j0, j1):
             nc.vector.tensor_tensor(
                 out=page[c][:].indirect(list3[:, j0 // GROUP:j1 // GROUP]), in0=values, in1=gain, op=ALU.mult,
             )
-
-        def slice_residual(s):
-            flat = rm_slice[s][:].rearrange("p c j -> p (c j)")
-            return [turn_residual(flat[:, i * BANK:(i + 1) * BANK]) for i in range(2)]
-
-        def slice_features(s, residual_t, y):
-            return [features([(c, 2 * s + half) for c in (2 * i, 2 * i + 1) for half in range(2)], residual_t[i], y[i]) for i in range(2)]
 
         def place_slice(s, c, y):
             place(c, y[c // 2][:, c % 2 * SLICE:(c % 2 + 1) * SLICE], gain[:, s * SLICE:(s + 1) * SLICE], s * SLICE, (s + 1) * SLICE)
@@ -251,6 +256,12 @@ def tile_list_proof_impression_judge_kernel(
         quantise_w1(0, 0)
         quantise_w1(0, 1)
         quantise_w1(1, 0)
+        for a in range(2):
+            for r in range(2):
+                nc.scalar.dma_start(
+                    out=v_scales[:].bitcast(I32)[4 * a + 2 + r:P:32, :],
+                    in_=v_scales_picked[:].bitcast(I32)[4 * a + GROUP + r:P:32, :],
+                )
         v_codes = {(a, h): gather(f"v_codes_{a}{h}", v_window[a], list1, U32, h * HALF, (h + 1) * HALF) for a in range(2) for h in range(2)}
         paper_readings(0, 0)
         paper_readings(0, 1)
@@ -260,16 +271,14 @@ def tile_list_proof_impression_judge_kernel(
         quantise_h(0, 0, larger_reading(0, 0))
         quantise_h(0, 1, larger_reading(0, 1))
         w3_q = [quantise_w3(b) for b in range(2)]
-        second_product(0)
-        y_slice = [slice_features(0, slice_residual(0), [ring.tile([P, BANK], F32, name="y", bufs=3) for i in range(2)])]
+        y_slice = [slice_features(0, [ring.tile([P, BANK], F32, name="y", bufs=3) for i in range(2)])]
         quantise_h(1, 0, larger_reading(1, 0))
         quantise_h(1, 1, larger_reading(1, 1))
-        second_product(1)
         for s in range(2):
             for b in range(2):
                 paper_readings(s + 2, b)
                 quantise_h(s + 2, b, larger_reading(s + 2, b))
-        y_slice.append(slice_features(1, slice_residual(1), [after_paper(f"y_1{b}", [P, BANK], 3, b, 1) for b in range(2)]))
+        y_slice.append(slice_features(1, [after_paper(f"y_1{b}", [P, BANK], 3, b, 1) for b in range(2)]))
         second_product(2)
         second_product(3)
         for s in range(2):

@@ -55,9 +55,7 @@ def tile_list_proof_impression_judge_kernel(
 
         def load_w3(slot, b):
             raw = rows_tile(slot, f"w3_raw_{b}", [P, PACK, N])
-            rows = w3[b * PASS:(b + 1) * PASS, :].rearrange("(u t e) n -> e u t n", t=PACK, e=2)
-            for e in range(2):
-                nc.sync.dma_start(out=raw[e:P:2, :, :], in_=rows[e])
+            nc.sync.dma_start(out=raw[:], in_=w3[b * PASS:(b + 1) * PASS, :].rearrange("(p t) n -> p t n", t=PACK))
             return raw
 
         def load_plane(queue, tile_i32, scales):
@@ -127,13 +125,13 @@ def tile_list_proof_impression_judge_kernel(
         nc.vector.tensor_copy(out=v_scales[:].bitcast(I32), in_=v_scales_picked[:].bitcast(I32))
         w2_codes = held("w2_codes", [P, 2 * H], U8)
         nc.vector.tensor_copy(
-            out=w2_codes[:].bitcast(I32).rearrange("p (b t u) -> p b t u", b=2, t=PACK),
-            in_=w2_raw[:].rearrange("p (b u t) -> p b t u", b=2, t=PACK),
+            out=w2_codes[:].bitcast(U16).rearrange("p (b t m) -> p b t m", b=2, t=PACK),
+            in_=w2_raw[:].bitcast(U16).rearrange("p (b m t) -> p b t m", b=2, t=PACK),
         )
         w2_plane = keep.tile([P, H], U8, name="w2_plane", tag="v_scale_window", align_bytes=64)
         nc.vector.tensor_copy(
-            out=w2_plane[:].bitcast(U16).rearrange("p (b t u) -> p b t u", b=2, t=PACK),
-            in_=w2_scale_raw[:].bitcast(U16).rearrange("p (b u t) -> p b t u", b=2, t=PACK),
+            out=w2_plane[:].rearrange("p (b t m) -> p b t m", b=2, t=PACK),
+            in_=w2_scale_raw[:].bitcast(U8).rearrange("p (b m t) -> p b t m", b=2, t=PACK),
         )
 
         w1_q, paper, h_q, product_t = {}, {}, {}, {}
@@ -142,8 +140,8 @@ def tile_list_proof_impression_judge_kernel(
             for pair in range(2):
                 rounded = ring.tile([P, 2 * PASS], BF16, name="w1_rounded", bufs=6, align_bytes=64)
                 nc.scalar.copy(
-                    out=rounded[:].rearrange("p (t u e i) -> p t u i e", t=2, e=2, i=PACK),
-                    in_=w1_raw[b, a][:].rearrange("p i (u t e) -> p t u i e", t=PACK, e=2)[:, 2 * pair:2 * pair + 2, :, :, :],
+                    out=rounded[:].rearrange("p (t m i) -> p m i t", t=2, i=PACK),
+                    in_=w1_raw[b, a][:].rearrange("p i (m t) -> p m i t", t=PACK)[:, :, :, 2 * pair:2 * pair + 2],
                 )
                 w1_q[b, a, pair] = quantise(f"w1_{b}{a}{pair}", rounded, 2 * P)
 
@@ -255,30 +253,28 @@ def tile_list_proof_impression_judge_kernel(
 
         quantise_w1(0, 0)
         quantise_w1(0, 1)
-        quantise_w1(1, 0)
         for a in range(2):
             for r in range(2):
                 nc.scalar.dma_start(
                     out=v_scales[:].bitcast(I32)[4 * a + 2 + r:P:32, :],
                     in_=v_scales_picked[:].bitcast(I32)[4 * a + GROUP + r:P:32, :],
                 )
+        quantise_w1(1, 0)
         v_codes = {(a, h): gather(f"v_codes_{a}{h}", v_window[a], list1, U32, h * HALF, (h + 1) * HALF) for a in range(2) for h in range(2)}
-        paper_readings(0, 0)
-        paper_readings(0, 1)
+        for s in range(SLICES):
+            paper_readings(s, 0)
         quantise_w1(1, 1)
-        paper_readings(1, 0)
-        paper_readings(1, 1)
-        quantise_h(0, 0, larger_reading(0, 0))
+        larger = [larger_reading(s, 0) for s in range(SLICES)]
+        paper_readings(0, 1)
+        quantise_h(0, 0, larger[0])
         quantise_h(0, 1, larger_reading(0, 1))
         w3_q = [quantise_w3(b) for b in range(2)]
         y_slice = [slice_features(0, [ring.tile([P, BANK], F32, name="y", bufs=3) for i in range(2)])]
-        quantise_h(1, 0, larger_reading(1, 0))
-        quantise_h(1, 1, larger_reading(1, 1))
-        for s in range(2):
-            for b in range(2):
-                paper_readings(s + 2, b)
-                quantise_h(s + 2, b, larger_reading(s + 2, b))
-        y_slice.append(slice_features(1, [after_paper(f"y_1{b}", [P, BANK], 3, b, 1) for b in range(2)]))
+        for s in range(1, SLICES):
+            paper_readings(s, 1)
+            quantise_h(s, 0, larger[s])
+            quantise_h(s, 1, larger_reading(s, 1))
+        y_slice.append(slice_features(1, [after_paper(f"y_1{b}", [P, BANK], 3, 1, b) for b in range(2)]))
         second_product(2)
         second_product(3)
         for s in range(2):

from contextlib import ExitStack

import concourse.mybir as mybir
from concourse.masks import make_identity

T, S, T2, K, K2, H, N = 2048, 1024, 2048, 1024, 512, 1024, 512
FLOPS = 2 * S * (K * H + K2 * H + H * N)

F32 = mybir.dt.float32
BF16 = mybir.dt.bfloat16
I32 = mybir.dt.int32
U32 = mybir.dt.uint32
U16 = mybir.dt.uint16
U8 = mybir.dt.uint8
FP8X4 = mybir.dt.float8_e4m3fn_x4
FP4X4 = mybir.dt.float4_e2m1fn_x4
ALU = mybir.AluOpType
ACT = mybir.ActivationFunctionType

P = 128
PACK = 4
PASS = P * PACK
SLICE = 256
SLICES = S // SLICE
GROUP = 16
BANK = 512


def tile_list_proof_impression_judge_kernel(
    tc, tab_words, tab_scales, tab2_words, tab2_scales, offs, offs2, offs3,
    w1, w2_words, w2_scales, w3, rm, page1, wgo, out,
):
    nc = tc.nc
    with ExitStack() as ctx:
        keep = ctx.enter_context(tc.tile_pool(name="keep", bufs=1))
        ring = ctx.enter_context(tc.tile_pool(name="ring", bufs=2))
        psum = ctx.enter_context(tc.psum_pool(name="psum", bufs=4))

        def held(name, shape, dtype):
            return keep.tile(shape, dtype, name=name, align_bytes=64)

        def rows_tile(slot, name, shape, dtype=F32):
            return keep.tile(shape, dtype, name=name, tag=f"rows_{slot}", align_bytes=64)

        def load_words(slot, name, words):
            window = rows_tile(slot, name, [P, T], U32)
            nc.sync.dma_start(out=window[:].bitcast(I32), in_=words.rearrange("p t i -> p (t i)").bitcast(I32))
            return window

        def load_w1(slot, b, a, queue=nc.sync):
            raw = rows_tile(slot, f"w1_raw_{b}{a}", [P, PACK, PASS])
            rows = w1[a * PASS:(a + 1) * PASS, b * PASS:(b + 1) * PASS]
            queue.dma_start(out=raw[:], in_=rows.rearrange("(p i) r -> p i r", i=PACK))
            return raw

        def load_w3(slot, b):
            raw = rows_tile(slot, f"w3_raw_{b}", [P, PACK, N])
            nc.sync.dma_start(out=raw[:], in_=w3[b * PASS:(b + 1) * PASS, :].rearrange("(p t) n -> p t n", t=PACK))
            return raw

        def load_plane(queue, tile_i32, scales):
            for d in range(4):
                queue.dma_start(out=tile_i32[32 * d:32 * d + 4, :], in_=scales[4 * d:4 * d + 4, :].bitcast(I32))

        def gather(name, window, offsets, dtype, j0=0, j1=S):
            picked = held(name, [P, j1 - j0], dtype)
            nc.vector.tensor_copy(out=picked[:], in_=window[:].indirect(offsets[:, j0 // GROUP:j1 // GROUP]))
            return picked

        def quantise(name, values, width):
            codes = held(f"{name}_codes", [P, width], U32)
            scales = held(f"{name}_scales", [P, width], U8)
            nc.vector.quantize_mx(out=codes[:].bitcast(FP8X4), scales=scales[:], in_=values[:])
            return codes, scales

        def after_paper(name, shape, s, b, pair):
            return keep.tile(shape, F32, name=name, tag=f"paper_{s}{b}{pair}", align_bytes=64)

        def load_f32(tile, rows):
            nc.sync.dma_start(out=tile[:], in_=rows)
            return tile

        v2_scale_window = held("v2_scale_window", [P, T], U8)
        nc.vector.memset(v2_scale_window[:].bitcast(I32), 0)
        v_scale_window = held("v_scale_window", [P, T], U8)
        nc.vector.memset(v_scale_window[:].bitcast(I32), 0)
        w2_scale_raw = held("w2_scale_raw", [P, H // 4], I32)
        nc.gpsimd.memset(w2_scale_raw[:], 0)

        list2 = held("list2", [P, S // GROUP], U16)
        nc.sync.dma_start(list2[:], offs2)
        v2_window = load_words(0, "v2_window", tab2_words[0])
        w1_raw = {(0, 0): load_w1(1, 0, 0)}
        list1 = held("list1", [P, S // GROUP], U16)
        nc.sync.dma_start(list1[:], offs)
        load_plane(nc.scalar, v2_scale_window[:].bitcast(I32), tab2_scales[0])
        for a in range(2):
            for r in range(2):
                nc.scalar.dma_start(out=v_scale_window[:].bitcast(I32)[4 * a + r:P:GROUP, :], in_=tab_scales[a, r:16:2, :].bitcast(I32))
        load_plane(nc.gpsimd, w2_scale_raw[:], w2_scales[0])
        w1_raw[0, 1] = load_w1(2, 0, 1)
        w1_raw[1, 0] = load_w1(5, 1, 0)
        w2_raw = held("w2_raw", [P, H // 2], I32)
        nc.sync.dma_start(out=w2_raw[:], in_=w2_words[0].bitcast(I32))
        v_window = [load_words(3 + a, f"v_window_{a}", tab_words[a]) for a in range(2)]
        w1_raw[1, 1] = load_w1(1, 1, 1)
        w3_raw = [load_w3(2, 0), load_w3(0, 1)]
        rm_rows = rm.rearrange("(c p) j -> p c j", p=P)
        rm_slice = [load_f32(held("rm_slice_0", [P, N // P, SLICE], F32), rm_rows[:, :, 0:SLICE])]
        gain = load_f32(held("gain", [P, S], F32), wgo)
        list3 = held("list3", [P, S // GROUP], U16)
        nc.sync.dma_start(list3[:], offs3)
        page = [load_f32(rows_tile(5, "page_0", [P, T2]), page1[0:P, :])]
        rm_slice.append(load_f32(held("rm_slice_1", [P, N // P, SLICE], F32), rm_rows[:, :, SLICE:2 * SLICE]))
        page += [load_f32(rows_tile((5, 3, 4, 1)[c], f"page_{c}", [P, T2]), page1[c * P:(c + 1) * P, :]) for c in range(1, N // P)]
        rm_rest = load_f32(held("rm_rest", [P, N // P, S // 2], F32), rm_rows[:, :, S // 2:S])
        identity = held("identity", [P, P], F32)
        make_identity(nc, identity[:])

        HALF = S // 2
        v2_codes = [gather(f"v2_codes_{h}", v2_window, list2, U32, h * HALF, (h + 1) * HALF) for h in range(2)]
        v2_scales = [gather(f"v2_scales_{h}", v2_scale_window, list2, U8, h * HALF, (h + 1) * HALF) for h in range(2)]
        v_scales_picked = gather("v_scales_picked", v_scale_window, list1, U8)
        v_scales = held("v_scales", [P, S], U8)
        nc.vector.tensor_copy(out=v_scales[:].bitcast(I32), in_=v_scales_picked[:].bitcast(I32))
        w2_codes = held("w2_codes", [P, 2 * H], U8)
        nc.vector.tensor_copy(
            out=w2_codes[:].bitcast(U16).rearrange("p (b t m) -> p b t m", b=2, t=PACK),
            in_=w2_raw[:].bitcast(U16).rearrange("p (b m t) -> p b t m", b=2, t=PACK),
        )
        w2_plane = keep.tile([P, H], U8, name="w2_plane", tag="v_scale_window", align_bytes=64)
        nc.vector.tensor_copy(
            out=w2_plane[:].rearrange("p (b t m) -> p b t m", b=2, t=PACK),
            in_=w2_scale_raw[:].bitcast(U8).rearrange("p (b m t) -> p b t m", b=2, t=PACK),
        )

        w1_q, paper, h_q, product_t = {}, {}, {}, {}

        def quantise_w1(b, a):
            for pair in range(2):
                rounded = ring.tile([P, 2 * PASS], BF16, name="w1_rounded", bufs=6, align_bytes=64)
                nc.scalar.copy(
                    out=rounded[:].rearrange("p (t m i) -> p m i t", t=2, i=PACK),
                    in_=w1_raw[b, a][:].rearrange("p i (m t) -> p m i t", t=PACK)[:, :, :, 2 * pair:2 * pair + 2],
                )
                w1_q[b, a, pair] = quantise(f"w1_{b}{a}{pair}", rounded, 2 * P)

        def quantise_w3(b):
            rounded = ring.tile([P, PACK * N], BF16, name="w3_rounded", bufs=2, align_bytes=64)
            nc.vector.tensor_copy(
                out=rounded[:].rearrange("p (c i t) -> p c t i", i=4, t=PACK),
                in_=w3_raw[b][:].rearrange("p t (c i) -> p c t i", i=4),
            )
            return quantise(f"w3_{b}", rounded, N)

        def paper_readings(s, b):
            cols = slice(s % 2 * SLICE, (s % 2 + 1) * SLICE)
            for pair in range(2):
                bank = psum.tile([P, 2, SLICE], F32, name="paper_bank", bufs=3)
                for t in range(2):
                    r0 = b * PASS + (2 * pair + t) * P
                    nc.tensor.matmul_mx(
                        out=bank[:, t, :],
                        lhsT=w2_codes[:, 2 * r0:2 * (r0 + P)].bitcast(FP4X4), lhsT_scale=w2_plane[:, r0:r0 + P],
                        rhs=v2_codes[s // 2][:, cols].bitcast(FP8X4), rhs_scale=v2_scales[s // 2][:, cols],
                        start=True, stop=True,
                    )
                paper[s, b, pair] = after_paper(f"paper_{s}{b}{pair}", [P, 2, SLICE], s, b, pair)
                nc.scalar.copy(out=paper[s, b, pair][:], in_=bank[:])

        def larger_reading(s, b):
            cols = slice(s * SLICE, (s + 1) * SLICE)
            larger = ring.tile([P, PACK, SLICE], F32, name="larger", bufs=4)
            for pair in range(2):
                bank = psum.tile([P, 2, SLICE], F32, name="sort_bank", bufs=3)
                for t in range(2):
                    for a in range(2):
                        codes, scales = w1_q[b, a, pair]
                        nc.tensor.matmul_mx(
                            out=bank[:, t, :],
                            lhsT=codes[:, t * P:(t + 1) * P].bitcast(FP8X4), lhsT_scale=scales[:, t * P:(t + 1) * P],
                            rhs=v_codes[a, s // 2][:, s % 2 * SLICE:(s % 2 + 1) * SLICE].bitcast(FP8X4), rhs_scale=v_scales[4 * a:P, cols],
                            start=(a == 0), stop=(a == 1),
                        )
                nc.vector.tensor_tensor(
                    out=larger[:, 2 * pair:2 * pair + 2, :], in0=bank[:], in1=paper[s, b, pair][:], op=ALU.max,
                )
            return larger

        def quantise_h(s, b, larger):
            h = ring.tile([P, PACK * SLICE], BF16, name="h", bufs=4, align_bytes=64)
            nc.scalar.activation(
                out=h[:].rearrange("p (c i t) -> p c t i", i=2, t=PACK),
                in_=larger[:].rearrange("p t (c i) -> p c t i", i=2), func=ACT.Abs,
            )
            h_q[s, b] = quantise(f"h_{s}{b}", h, SLICE)

        def second_product(s):
            for half in range(2):
                cols = slice(half * P, (half + 1) * P)
                bank = psum.tile([P, N], F32, name="late_bank", bufs=2)
                for b in range(2):
                    nc.tensor.matmul_mx(
                        out=bank[:],
                        lhsT=h_q[s, b][0][:, cols].bitcast(FP8X4), lhsT_scale=h_q[s, b][1][:, cols],
                        rhs=w3_q[b][0][:].bitcast(FP8X4), rhs_scale=w3_q[b][1][:],
                        start=(b == 0), stop=(b == 1),
                    )
                product_t[2 * s + half] = held(f"product_t_{s}{half}", [P, N], F32)
                nc.scalar.copy(out=product_t[2 * s + half][:], in_=bank[:])

        def turn_residual(residual):
            bank = psum.tile([P, BANK], F32, name="late_bank", bufs=2)
            for i in range(BANK // P):
                nc.tensor.transpose(bank[:, i * P:(i + 1) * P], residual[:, i * P:(i + 1) * P], identity[:])
            residual_t = ring.tile([P, BANK], F32, name="residual_t", bufs=4)
            nc.scalar.copy(out=residual_t[:], in_=bank[:])
            return residual_t

        def features(blocks, residual_t, y):
            bank = psum.tile([P, BANK], F32, name="late_bank", bufs=2)
            for i, (c, jt) in enumerate(blocks):
                cols = slice(i * P, (i + 1) * P)
                nc.tensor.matmul(bank[:, cols], residual_t[:, cols], identity[:], start=True, stop=False, is_transpose=True)
                nc.tensor.matmul(bank[:, cols], product_t[jt][:, c * P:(c + 1) * P], identity[:], start=False, stop=True, is_transpose=True)
            nc.scalar.activation(out=y[:], in_=bank[:], func=ACT.Tanh)
            return y

        def slice_features(s, y):
            for i in range(2):
                bank = psum.tile([P, 2, SLICE], F32, name="late_bank", bufs=2)
                for k in range(2):
                    cols = slice((2 * i + k) * P, (2 * i + k + 1) * P)
                    for b in range(2):
                        nc.tensor.matmul_mx(
                            out=bank[:, k, :],
                            lhsT=w3_q[b][0][:, cols].bitcast(FP8X4), lhsT_scale=w3_q[b][1][:, cols],
                            rhs=h_q[s, b][0][:].bitcast(FP8X4), rhs_scale=h_q[s, b][1][:],
                            start=(b == 0), stop=(b == 1),
                        )
                summed = ring.tile([P, 2, SLICE], F32, name="summed")
                nc.vector.tensor_tensor(out=summed[:], in0=bank[:], in1=rm_slice[s][:, 2 * i:2 * i + 2, :], op=ALU.add)
                nc.scalar.activation(out=y[i][:], in_=summed[:].rearrange("p k j -> p (k j)"), func=ACT.Tanh)
            return y

        def place(c, values, gain, j0, j1):
            nc.vector.tensor_tensor(
                out=page[c][:].indirect(list3[:, j0 // GROUP:j1 // GROUP]), in0=values, in1=gain, op=ALU.mult,
            )

        def place_slice(s, c, y):
            place(c, y[c // 2][:, c % 2 * SLICE:(c % 2 + 1) * SLICE], gain[:, s * SLICE:(s + 1) * SLICE], s * SLICE, (s + 1) * SLICE)

        quantise_w1(0, 0)
        quantise_w1(0, 1)
        for a in range(2):
            for r in range(2):
                nc.scalar.dma_start(
                    out=v_scales[:].bitcast(I32)[4 * a + 2 + r:P:32, :],
                    in_=v_scales_picked[:].bitcast(I32)[4 * a + GROUP + r:P:32, :],
                )
        quantise_w1(1, 0)
        v_codes = {(a, h): gather(f"v_codes_{a}{h}", v_window[a], list1, U32, h * HALF, (h + 1) * HALF) for a in range(2) for h in range(2)}
        for s in range(SLICES):
            paper_readings(s, 0)
        quantise_w1(1, 1)
        larger = [larger_reading(s, 0) for s in range(SLICES)]
        paper_readings(0, 1)
        quantise_h(0, 0, larger[0])
        quantise_h(0, 1, larger_reading(0, 1))
        w3_q = [quantise_w3(b) for b in range(2)]
        y_slice = [slice_features(0, [ring.tile([P, BANK], F32, name="y", bufs=3) for i in range(2)])]
        for s in range(1, SLICES):
            paper_readings(s, 1)
            quantise_h(s, 0, larger[s])
            quantise_h(s, 1, larger_reading(s, 1))
        y_slice.append(slice_features(1, [after_paper(f"y_1{b}", [P, BANK], 3, 1, b) for b in range(2)]))
        second_product(2)
        second_product(3)
        for s in range(2):
            for c in range(N // P):
                place_slice(s, c, y_slice[s])
        for c in range(N // P):
            y = features([(c, jt) for jt in range(4, 8)], turn_residual(rm_rest[:, c, :]), ring.tile([P, BANK], F32, name="y", bufs=3))
            place(c, y[:], gain[:, HALF:S], HALF, S)
            nc.sync.dma_start(out=out[c * P:(c + 1) * P, :], in_=page[c][:])
